import numpy as np
import ml_dtypes


def mxq(x, axis, fmt="e4m3"):
    dtype, down = {"e4m3": (ml_dtypes.float8_e4m3fn, 7), "e5m2": (ml_dtypes.float8_e5m2, 14)}[fmt]
    v = np.moveaxis(np.asarray(x, np.float32).astype(ml_dtypes.bfloat16).astype(np.float64), axis, -1)
    blocks = v.reshape(v.shape[:-1] + (-1, 32))
    amax = np.abs(blocks).max(-1, keepdims=True)
    byte = np.maximum(np.where(amax > 0, np.frexp(amax)[1] - 1 + 127, 0) - down, 1)
    scale = np.exp2(byte - 127.0)
    codes = (blocks / scale).astype(np.float32).astype(dtype).astype(np.float64)
    return np.moveaxis((codes * scale).reshape(v.shape), -1, axis)


WIDE = False


def mx_kscale(k):
    if not WIDE:
        return np.ones(k)
    levels = np.array([30, -30])
    if k % 512:
        return np.exp2(np.random.permutation(np.resize(levels, k // 32))).repeat(32)
    a = np.empty((k // 512, 16))
    for p in range(k // 512):
        a[p, :8] = np.random.permutation(np.resize(levels, 8))
        for g in range(8):
            far = levels[np.abs(levels - a[p, g]) >= 10]
            a[p, g + 8] = far[np.random.randint(len(far))]
    return np.exp2(a.ravel()).repeat(32)


def f64(x):
    return np.asarray(x).astype(np.float64)


def striped(idx):
    return np.tile(np.asarray(idx).reshape(-1, 16).T, (8, 1)).astype(np.uint16)


def unstriped(offs):
    return offs[:16].T.reshape(-1).astype(np.int64)


E2M1 = np.array([0.0, 0.5, 1.0, 1.5, 2.0, 3.0, 4.0, 6.0, -0.0, -0.5, -1.0, -1.5, -2.0, -3.0, -4.0, -6.0])


def pack_weight(w, fmt):
    k, n = w.shape
    w = f64(np.asarray(w, np.float32).astype(ml_dtypes.bfloat16)).reshape(k // 32, 32, n)
    amax = np.abs(w).max(1)
    if fmt in ("e4m3", "e5m2"):
        byte = np.frexp(amax)[1] - 1 + 127 - (7 if fmt == "e4m3" else 14)
    else:
        mant, ex = np.frexp(amax / 6.0)
        byte = np.where(mant > 0.5, ex, ex - 1) + 127
    byte = np.clip(np.where(amax > 0, byte, 1), 1, 254)
    scaled = (w * np.exp2(127.0 - byte)[:, None, :]).reshape(k, n).astype(np.float32)
    by_word = np.ascontiguousarray(scaled.reshape(k // 512, 128, 4, n).transpose(0, 1, 3, 2))
    if fmt in ("e4m3", "e5m2"):
        words = by_word.astype(ml_dtypes.float8_e4m3fn if fmt == "e4m3" else ml_dtypes.float8_e5m2).view(np.uint8)
    else:
        c = by_word.astype(ml_dtypes.float4_e2m1fn).view(np.uint8) & 0xF
        words = (c[..., 0::2] | (c[..., 1::2] << 4)).reshape(k // 512, 128, 2 * n)
    return np.ascontiguousarray(words), np.ascontiguousarray(byte.astype(np.uint8).reshape(k // 512, 16, n))


def unpack_weight(words, scales, fmt):
    g, _, n = scales.shape
    words = np.ascontiguousarray(words).reshape(g, 128, n, -1)
    if fmt in ("e4m3", "e5m2"):
        vals = words.view(ml_dtypes.float8_e4m3fn if fmt == "e4m3" else ml_dtypes.float8_e5m2).astype(np.float64)
    else:
        nib = np.empty((g, 128, n, 4), np.uint8)
        nib[..., 0::2] = words & 0xF
        nib[..., 1::2] = words >> 4
        vals = E2M1[nib]
    vals = vals * np.repeat(np.exp2(scales.astype(np.float64) - 127.0), 8, axis=1)[..., None]
    return vals.transpose(0, 1, 3, 2).reshape(g * 512, n)


def sgn(shape):
    return np.random.uniform(0.5, 2.0, shape) * np.where(np.random.standard_normal(shape) < 0, -1.0, 1.0)


K, T, J, F, Z, Q, R, C, O, N = 512, 1024, 256, 512, 1024, 128, 512, 512, 256, 256


def setup_inputs():
    n = np.random.standard_normal
    idx = np.random.permutation(T)[:J]
    idx2 = np.random.permutation(Z)[:J]
    idx3 = np.random.permutation(C)[:J]
    idx4 = np.random.permutation(C)[:J]
    idx5 = np.random.permutation(C)[:O]
    idx6 = np.random.permutation(C)[:O]
    fk = mx_kscale(K)
    ff = mx_kscale(F)
    fr = mx_kscale(R)
    xtp = pack_weight(n((K, T)) / fk[:, None], "e4m3")
    xop = pack_weight(n((F, Z)) / ff[:, None], "e2m1")
    wp = pack_weight(n((K, Q)) * 1 / np.sqrt(K) * fk[:, None], "e2m1")
    w2p = pack_weight(n((F, Q)) * 1 / np.sqrt(F) * ff[:, None], "e5m2")
    wbp = pack_weight(n((R, N)) * 1 / np.sqrt(R) / fr[:, None], "e5m2")
    return {
        "xt_words": xtp[0],
        "xt_scales": xtp[1],
        "xo_words": xop[0],
        "xo_scales": xop[1],
        "w_words": wp[0],
        "w_scales": wp[1],
        "w2_words": w2p[0],
        "w2_scales": w2p[1],
        "sa": (np.random.uniform(0.5, 1.6, (Q, 1)) * fr[::4, None]).astype(np.float32),
        "sb": (sgn((Q, 1)) * fr[::4, None]).astype(np.float32),
        "wb_words": wbp[0],
        "wb_scales": wbp[1],
        "offs": striped(idx),
        "offs2": striped(idx2),
        "offs3": striped(idx3),
        "offs4": striped(idx4),
        "offs5": striped(idx5),
        "offs6": striped(idx6),
    }


def reference(xt_words, xt_scales, xo_words, xo_scales, w_words, w_scales, w2_words, w2_scales, sa, sb, wb_words, wb_scales, offs, offs2, offs3, offs4, offs5, offs6):
    idx = unstriped(offs)
    idx2 = unstriped(offs2)
    idx3 = unstriped(offs3)
    idx4 = unstriped(offs4)
    idx5 = unstriped(offs5)
    idx6 = unstriped(offs6)
    xtu = unpack_weight(xt_words, xt_scales, "e4m3")
    xou = unpack_weight(xo_words, xo_scales, "e2m1")
    wu = unpack_weight(w_words, w_scales, "e2m1")
    w2u = unpack_weight(w2_words, w2_scales, "e5m2")
    wbu = unpack_weight(wb_words, wb_scales, "e5m2")
    xtidxg = xtu[:, idx]
    a = wu.T @ xtidxg
    xoidx2g = xou[:, idx2]
    b = w2u.T @ xoidx2g
    pa = np.zeros((Q, C))
    pa[:, idx3] = a * f64(sa)
    pb = np.zeros((Q, C))
    pb[:, idx4] = b * f64(sb)
    v0 = pa[:, idx5]
    v1 = pb[:, idx5]
    v2 = pa[:, idx6]
    v3 = pb[:, idx6]
    hid = np.stack([v0, v1, v2, v3], axis=1).reshape(R, O)
    hidq = mxq(hid, 0, "e4m3")
    p = wbu.T @ hidq
    return p

@@ -1,0 +1,154 @@
+from contextlib import ExitStack
+
+import concourse.mybir as mybir
+
+F32 = mybir.dt.float32
+BF16 = mybir.dt.bfloat16
+I32 = mybir.dt.int32
+U32 = mybir.dt.uint32
+U16 = mybir.dt.uint16
+U8 = mybir.dt.uint8
+E4M3 = mybir.dt.float8_e4m3fn_x4
+E5M2 = mybir.dt.float8_e5m2_x4
+E2M1 = mybir.dt.float4_e2m1fn_x4
+COPY = mybir.ActivationFunctionType.Copy
+
+P = 128
+T, Z, J, Q, C, O, N = 1024, 1024, 256, 128, 512, 256, 256
+HALF = 128
+FLOPS = 2 * 512 * Q * J * 2 + 2 * 512 * N * O
+
+
+def tile_list_fourreads_kernel(tc, xt_words, xt_scales, xo_words, xo_scales, w_words, w_scales, w2_words, w2_scales,
+                                    sa, sb, wb_words, wb_scales, offs, offs2, offs3, offs4, offs5, offs6, out):
+    nc = tc.nc
+    with ExitStack() as ctx:
+        keep = ctx.enter_context(tc.tile_pool(name="keep", bufs=1))
+        psum = ctx.enter_context(tc.psum_pool(name="psum", bufs=1))
+
+        def tile(name, shape, dtype, tag=None):
+            return keep.tile(shape, dtype, name=name, tag=tag or name, align_bytes=64)
+
+        def zeroed_plane(name, width, tag=None):
+            plane = tile(name, [P, width], U8, tag)
+            nc.vector.memset(plane[:].bitcast(I32), 0)
+            return plane
+
+        def load_list(name, src):
+            lst = keep.tile([P, J // 16], U16, name=name)
+            nc.sync.dma_start(lst[:], src)
+            return lst
+
+        def load_words(name, src, shape, dtype, queue=nc.sync, tag=None):
+            words = tile(name, shape, dtype, tag)
+            queue.dma_start(words[:].bitcast(I32), src.bitcast(I32))
+            return words
+
+        def load_scale_rows(name, src, queue=nc.sync):
+            width = src.shape[2]
+            rows = tile(name, [4, 4, width // 4], I32)
+            queue.dma_start(rows[:], src[0].rearrange("(g r) n -> r g n", r=4).bitcast(I32))
+            return rows
+
+        def spread(plane, rows):
+            for g in range(4):
+                nc.vector.tensor_copy(plane[32 * g : 32 * g + 4, :].bitcast(I32), rows[:, g, :])
+
+        def half_of(lst, h):
+            return lst[:, h * (HALF // 16) : (h + 1) * (HALF // 16)]
+
+        xo_plane = zeroed_plane("xo_plane", Z)
+        w2_plane = zeroed_plane("w2_plane", Q, "weight_plane")
+        xt_plane = zeroed_plane("xt_plane", T)
+
+        sb_t = tile("sb_t", [P, 1], F32)
+        nc.gpsimd.dma_start(sb_t[:], sb)
+        pb = tile("pb", [P, C], F32)
+        nc.gpsimd.memset(pb[:], 0.0)
+        pa = tile("pa", [P, C], F32)
+        nc.gpsimd.memset(pa[:], 0.0)
+
+        w2_rows = load_scale_rows("w2_rows", w2_scales, nc.scalar)
+        xo_w = load_words("xo_w", xo_words[0], [P, Z], U16)
+        l2 = load_list("l2", offs2)
+        for g in range(4):
+            queue = nc.scalar if g < 2 else nc.sync
+            queue.dma_start(xo_plane[32 * g : 32 * g + 4, :].bitcast(I32), xo_scales[0, 4 * g : 4 * g + 4, :].bitcast(I32))
+        w2_w = load_words("w2_w", w2_words[0].rearrange("p n t -> p (n t)"), [P, Q], U32, nc.scalar, "w2_words")
+
+        l4 = load_list("l4", offs4)
+        l5 = load_list("l5", offs5)
+        l1 = load_list("l1", offs)
+        for g in range(4):
+            nc.sync.dma_start(xt_plane[32 * g : 32 * g + 4, :].bitcast(I32), xt_scales[0, 4 * g : 4 * g + 4, :].bitcast(I32))
+        xt_w = load_words("xt_w", xt_words[0].rearrange("p n t -> p (n t)"), [P, T], U32)
+        w_rows = load_scale_rows("w_rows", w_scales)
+        w_w = load_words("w_w", w_words[0], [P, 2 * Q], U8)
+        l6 = load_list("l6", offs6)
+        l3 = load_list("l3", offs3)
+        sa_t = tile("sa_t", [P, 1], F32)
+        nc.sync.dma_start(sa_t[:], sa)
+        wb_w = load_words("wb_w", wb_words[0].rearrange("p n t -> p (n t)"), [P, N], U32)
+        wb_rows = load_scale_rows("wb_rows", wb_scales)
+
+        spread(w2_plane, w2_rows)
+        b_psum = []
+        for h in range(2):
+            g_words = tile("xo_gw%d" % h, [P, HALF], U16, "picked_words" if h == 1 else None)
+            g_scales = tile("xo_gs%d" % h, [P, HALF], U8, "picked_scales" if h == 1 else None)
+            nc.vector.tensor_copy(g_words[:], xo_w[:].indirect(half_of(l2, h)))
+            nc.vector.tensor_copy(g_scales[:], xo_plane[:].indirect(half_of(l2, h)))
+            acc = psum.tile([P, HALF], F32, name="b_acc%d" % h)
+            nc.tensor.matmul_mx(out=acc[:], lhsT=w2_w[:].bitcast(E5M2), lhsT_scale=w2_plane[:],
+                                rhs=g_words[:].bitcast(E2M1), rhs_scale=g_scales[:], start=True, stop=True)
+            b_psum.append(acc)
+        b0 = tile("b0", [P, HALF], F32)
+        nc.scalar.activation(b0[:], b_psum[0][:], COPY)
+        nc.scalar.activation(pb[:].indirect(half_of(l4, 0)), b0[:], COPY, scale=sb_t[:])
+        b1 = tile("b1", [P, HALF], F32)
+        nc.vector.tensor_copy(b1[:], b_psum[1][:])
+        nc.scalar.activation(pb[:].indirect(half_of(l4, 1)), b1[:], COPY, scale=sb_t[:])
+
+        hid = [tile("hid%d" % h, [P, 4 * HALF], BF16) for h in range(2)]
+        for h in range(2):
+            nc.scalar.activation(hid[h][:, 1 : 4 * HALF : 4], pb[:].indirect(half_of(l5, h)), COPY)
+        for h in range(2):
+            nc.scalar.activation(hid[h][:, 3 : 4 * HALF : 4], pb[:].indirect(half_of(l6, h)), COPY)
+
+        xt_gs = tile("xt_gs", [P, J], U8, "picked_scales")
+        nc.vector.tensor_copy(xt_gs[:], xt_plane[:].indirect(l1[:]))
+        w_plane = zeroed_plane("w_plane", Q, "weight_plane")
+        spread(w_plane, w_rows)
+        a_sb = tile("a_sb", [P, J], F32)
+        for h in range(2):
+            cols = slice(h * HALF, (h + 1) * HALF)
+            xt_gw = tile("xt_gw%d" % h, [P, HALF], U32, "picked_words" if h == 0 else "w2_words")
+            nc.vector.tensor_copy(xt_gw[:], xt_w[:].indirect(half_of(l1, h)))
+            a_acc = psum.tile([P, HALF], F32, name="a_acc%d" % h)
+            nc.tensor.matmul_mx(out=a_acc[:], lhsT=w_w[:].bitcast(E2M1), lhsT_scale=w_plane[:],
+                                rhs=xt_gw[:].bitcast(E4M3), rhs_scale=xt_gs[:, cols], start=True, stop=True)
+            nc.vector.tensor_copy(a_sb[:, cols], a_acc[:])
+        nc.scalar.activation(pa[:].indirect(l3[:]), a_sb[:], COPY, scale=sa_t[:])
+        wb_plane = zeroed_plane("wb_plane", N, "weight_plane")
+        spread(wb_plane, wb_rows)
+
+        for h in range(2):
+            nc.scalar.activation(hid[h][:, 0 : 4 * HALF : 4], pa[:].indirect(half_of(l5, h)), COPY)
+        for h in range(2):
+            nc.scalar.activation(hid[h][:, 2 : 4 * HALF : 4], pa[:].indirect(half_of(l6, h)), COPY)
+        for h in range(2):
+            codes = tile("hid_codes%d" % h, [P, HALF], U32)
+            scales = tile("hid_scales%d" % h, [P, HALF], U8)
+            nc.vector.quantize_mx(out=codes[:].bitcast(E4M3), scales=scales[:], in_=hid[h][:])
+            for t in range(2):
+                rows = slice(t * P, (t + 1) * P)
+                acc = psum.tile([P, HALF], F32, name="o_acc%d%d" % (h, t))
+                nc.tensor.matmul_mx(out=acc[:], lhsT=wb_w[:, rows].bitcast(E5M2), lhsT_scale=wb_plane[:, rows],
+                                    rhs=codes[:].bitcast(E4M3), rhs_scale=scales[:], start=True, stop=True)
+                res = tile("res%d%d" % (h, t), [P, HALF], F32)
+                if h == 1 and t == 1:
+                    nc.scalar.activation(res[:], acc[:], COPY)
+                    nc.scalar.dma_start(out[rows, h * HALF : (h + 1) * HALF], res[:])
+                else:
+                    nc.vector.tensor_copy(res[:], acc[:])
+                    nc.sync.dma_start(out[rows, h * HALF : (h + 1) * HALF], res[:])

@@ -44,57 +44,60 @@ def tile_list_fourreads_kernel(tc, xt_words, xt_scales, xo_words, xo_scales, w_w
             queue.dma_start(words[:].bitcast(I32), src.bitcast(I32))
             return words
 
-        def load_scale_rows(name, src, queue=nc.sync):
+        def load_scale_rows(name, src, queue=nc.sync, tag=None):
             width = src.shape[2]
-            rows = tile(name, [4, 4, width // 4], I32)
+            rows = tile(name, [4, 4, width // 4], I32, tag)
             queue.dma_start(rows[:], src[0].rearrange("(g r) n -> r g n", r=4).bitcast(I32))
             return rows
 
         def spread(plane, rows):
-            for g in range(4):
+            for g in (1, 2, 3, 0):
                 nc.vector.tensor_copy(plane[32 * g : 32 * g + 4, :].bitcast(I32), rows[:, g, :])
+
+        def load_plane(plane, src, queues):
+            for g in range(4):
+                queues[g].dma_start(plane[32 * g : 32 * g + 4, :].bitcast(I32), src[0, 4 * g : 4 * g + 4, :].bitcast(I32))
 
         def half_of(lst, h):
             return lst[:, h * (HALF // 16) : (h + 1) * (HALF // 16)]
 
         xo_plane = zeroed_plane("xo_plane", Z)
-        w2_plane = zeroed_plane("w2_plane", Q, "weight_plane")
+        w2_plane = zeroed_plane("w2_plane", Q)
         xt_plane = zeroed_plane("xt_plane", T)
+        w_plane = zeroed_plane("w_plane", Q)
+        wb_plane = zeroed_plane("wb_plane", N)
 
         sb_t = tile("sb_t", [P, 1], F32)
         nc.gpsimd.dma_start(sb_t[:], sb)
         pb = tile("pb", [P, C], F32)
-        nc.gpsimd.memset(pb[:], 0.0)
+        nc.vector.memset(pb[:], 0.0)
         pa = tile("pa", [P, C], F32)
         nc.gpsimd.memset(pa[:], 0.0)
 
-        w2_rows = load_scale_rows("w2_rows", w2_scales, nc.scalar)
+        w2_rows = load_scale_rows("w2_rows", w2_scales, nc.scalar, "picked_words")
         xo_w = load_words("xo_w", xo_words[0], [P, Z], U16)
         l2 = load_list("l2", offs2)
-        for g in range(4):
-            queue = nc.scalar if g < 2 else nc.sync
-            queue.dma_start(xo_plane[32 * g : 32 * g + 4, :].bitcast(I32), xo_scales[0, 4 * g : 4 * g + 4, :].bitcast(I32))
+        load_plane(xo_plane, xo_scales, [nc.scalar, nc.scalar, nc.sync, nc.sync])
         w2_w = load_words("w2_w", w2_words[0].rearrange("p n t -> p (n t)"), [P, Q], U32, nc.scalar, "w2_words")
 
         l4 = load_list("l4", offs4)
         l5 = load_list("l5", offs5)
         l1 = load_list("l1", offs)
-        for g in range(4):
-            nc.sync.dma_start(xt_plane[32 * g : 32 * g + 4, :].bitcast(I32), xt_scales[0, 4 * g : 4 * g + 4, :].bitcast(I32))
+        load_plane(xt_plane, xt_scales, [nc.sync] * 4)
         xt_w = load_words("xt_w", xt_words[0].rearrange("p n t -> p (n t)"), [P, T], U32)
-        w_rows = load_scale_rows("w_rows", w_scales)
+        load_plane(w_plane, w_scales, [nc.sync] * 4)
         w_w = load_words("w_w", w_words[0], [P, 2 * Q], U8)
         l6 = load_list("l6", offs6)
         l3 = load_list("l3", offs3)
         sa_t = tile("sa_t", [P, 1], F32)
         nc.sync.dma_start(sa_t[:], sa)
         wb_w = load_words("wb_w", wb_words[0].rearrange("p n t -> p (n t)"), [P, N], U32)
-        wb_rows = load_scale_rows("wb_rows", wb_scales)
+        load_plane(wb_plane, wb_scales, [nc.sync] * 4)
 
         spread(w2_plane, w2_rows)
         b_psum = []
         for h in range(2):
-            g_words = tile("xo_gw%d" % h, [P, HALF], U16, "picked_words" if h == 1 else None)
+            g_words = tile("xo_gw%d" % h, [P, HALF], U16, "picked_words")
             g_scales = tile("xo_gs%d" % h, [P, HALF], U8, "picked_scales" if h == 1 else None)
             nc.vector.tensor_copy(g_words[:], xo_w[:].indirect(half_of(l2, h)))
             nc.vector.tensor_copy(g_scales[:], xo_plane[:].indirect(half_of(l2, h)))
@@ -117,8 +120,6 @@ def tile_list_fourreads_kernel(tc, xt_words, xt_scales, xo_words, xo_scales, w_w
 
         xt_gs = tile("xt_gs", [P, J], U8, "picked_scales")
         nc.vector.tensor_copy(xt_gs[:], xt_plane[:].indirect(l1[:]))
-        w_plane = zeroed_plane("w_plane", Q, "weight_plane")
-        spread(w_plane, w_rows)
         a_sb = tile("a_sb", [P, J], F32)
         for h in range(2):
             cols = slice(h * HALF, (h + 1) * HALF)
@@ -129,8 +130,6 @@ def tile_list_fourreads_kernel(tc, xt_words, xt_scales, xo_words, xo_scales, w_w
                                 rhs=xt_gw[:].bitcast(E4M3), rhs_scale=xt_gs[:, cols], start=True, stop=True)
             nc.vector.tensor_copy(a_sb[:, cols], a_acc[:])
         nc.scalar.activation(pa[:].indirect(l3[:]), a_sb[:], COPY, scale=sa_t[:])
-        wb_plane = zeroed_plane("wb_plane", N, "weight_plane")
-        spread(wb_plane, wb_rows)
 
         for h in range(2):
             nc.scalar.activation(hid[h][:, 0 : 4 * HALF : 4], pa[:].indirect(half_of(l5, h)), COPY)

from contextlib import ExitStack

import concourse.mybir as mybir

F32 = mybir.dt.float32
BF16 = mybir.dt.bfloat16
I32 = mybir.dt.int32
U32 = mybir.dt.uint32
U16 = mybir.dt.uint16
U8 = mybir.dt.uint8
E4M3 = mybir.dt.float8_e4m3fn_x4
E5M2 = mybir.dt.float8_e5m2_x4
E2M1 = mybir.dt.float4_e2m1fn_x4
COPY = mybir.ActivationFunctionType.Copy

P = 128
T, Z, J, Q, C, O, N = 1024, 1024, 256, 128, 512, 256, 256
HALF = 128
FLOPS = 2 * 512 * Q * J * 2 + 2 * 512 * N * O


def tile_list_fourreads_kernel(tc, xt_words, xt_scales, xo_words, xo_scales, w_words, w_scales, w2_words, w2_scales,
                                    sa, sb, wb_words, wb_scales, offs, offs2, offs3, offs4, offs5, offs6, out):
    nc = tc.nc
    with ExitStack() as ctx:
        keep = ctx.enter_context(tc.tile_pool(name="keep", bufs=1))
        psum = ctx.enter_context(tc.psum_pool(name="psum", bufs=1))

        def tile(name, shape, dtype, tag=None):
            return keep.tile(shape, dtype, name=name, tag=tag or name, align_bytes=64)

        def zeroed_plane(name, width, tag=None):
            plane = tile(name, [P, width], U8, tag)
            nc.vector.memset(plane[:].bitcast(I32), 0)
            return plane

        def load_list(name, src):
            lst = keep.tile([P, J // 16], U16, name=name)
            nc.sync.dma_start(lst[:], src)
            return lst

        def load_words(name, src, shape, dtype, queue=nc.sync, tag=None):
            words = tile(name, shape, dtype, tag)
            queue.dma_start(words[:].bitcast(I32), src.bitcast(I32))
            return words

        def load_scale_rows(name, src, queue=nc.sync, tag=None):
            width = src.shape[2]
            rows = tile(name, [4, 4, width // 4], I32, tag)
            queue.dma_start(rows[:], src[0].rearrange("(g r) n -> r g n", r=4).bitcast(I32))
            return rows

        def spread(plane, rows):
            for g in (1, 2, 3, 0):
                nc.vector.tensor_copy(plane[32 * g : 32 * g + 4, :].bitcast(I32), rows[:, g, :])

        def load_plane(plane, src, queues):
            for g in range(4):
                queues[g].dma_start(plane[32 * g : 32 * g + 4, :].bitcast(I32), src[0, 4 * g : 4 * g + 4, :].bitcast(I32))

        def half_of(lst, h):
            return lst[:, h * (HALF // 16) : (h + 1) * (HALF // 16)]

        xo_plane = zeroed_plane("xo_plane", Z)
        w2_plane = zeroed_plane("w2_plane", Q)
        xt_plane = zeroed_plane("xt_plane", T)
        w_plane = zeroed_plane("w_plane", Q)
        wb_plane = zeroed_plane("wb_plane", N)

        sb_t = tile("sb_t", [P, 1], F32)
        nc.gpsimd.dma_start(sb_t[:], sb)
        pb = tile("pb", [P, C], F32)
        nc.vector.memset(pb[:], 0.0)
        pa = tile("pa", [P, C], F32)
        nc.gpsimd.memset(pa[:], 0.0)

        w2_rows = load_scale_rows("w2_rows", w2_scales, nc.scalar, "picked_words")
        xo_w = load_words("xo_w", xo_words[0], [P, Z], U16)
        l2 = load_list("l2", offs2)
        load_plane(xo_plane, xo_scales, [nc.scalar, nc.scalar, nc.sync, nc.sync])
        w2_w = load_words("w2_w", w2_words[0].rearrange("p n t -> p (n t)"), [P, Q], U32, nc.scalar, "w2_words")

        l4 = load_list("l4", offs4)
        l5 = load_list("l5", offs5)
        l1 = load_list("l1", offs)
        load_plane(xt_plane, xt_scales, [nc.sync] * 4)
        xt_w = load_words("xt_w", xt_words[0].rearrange("p n t -> p (n t)"), [P, T], U32)
        load_plane(w_plane, w_scales, [nc.sync] * 4)
        w_w = load_words("w_w", w_words[0], [P, 2 * Q], U8)
        l6 = load_list("l6", offs6)
        l3 = load_list("l3", offs3)
        sa_t = tile("sa_t", [P, 1], F32)
        nc.sync.dma_start(sa_t[:], sa)
        wb_w = load_words("wb_w", wb_words[0].rearrange("p n t -> p (n t)"), [P, N], U32)
        load_plane(wb_plane, wb_scales, [nc.sync] * 4)

        spread(w2_plane, w2_rows)
        b_psum = []
        for h in range(2):
            g_words = tile("xo_gw%d" % h, [P, HALF], U16, "picked_words")
            g_scales = tile("xo_gs%d" % h, [P, HALF], U8, "picked_scales" if h == 1 else None)
            nc.vector.tensor_copy(g_words[:], xo_w[:].indirect(half_of(l2, h)))
            nc.vector.tensor_copy(g_scales[:], xo_plane[:].indirect(half_of(l2, h)))
            acc = psum.tile([P, HALF], F32, name="b_acc%d" % h)
            nc.tensor.matmul_mx(out=acc[:], lhsT=w2_w[:].bitcast(E5M2), lhsT_scale=w2_plane[:],
                                rhs=g_words[:].bitcast(E2M1), rhs_scale=g_scales[:], start=True, stop=True)
            b_psum.append(acc)
        b0 = tile("b0", [P, HALF], F32)
        nc.scalar.activation(b0[:], b_psum[0][:], COPY)
        nc.scalar.activation(pb[:].indirect(half_of(l4, 0)), b0[:], COPY, scale=sb_t[:])
        b1 = tile("b1", [P, HALF], F32)
        nc.vector.tensor_copy(b1[:], b_psum[1][:])
        nc.scalar.activation(pb[:].indirect(half_of(l4, 1)), b1[:], COPY, scale=sb_t[:])

        hid = [tile("hid%d" % h, [P, 4 * HALF], BF16) for h in range(2)]
        for h in range(2):
            nc.scalar.activation(hid[h][:, 1 : 4 * HALF : 4], pb[:].indirect(half_of(l5, h)), COPY)
        for h in range(2):
            nc.scalar.activation(hid[h][:, 3 : 4 * HALF : 4], pb[:].indirect(half_of(l6, h)), COPY)

        xt_gs = tile("xt_gs", [P, J], U8, "picked_scales")
        nc.vector.tensor_copy(xt_gs[:], xt_plane[:].indirect(l1[:]))
        a_sb = tile("a_sb", [P, J], F32)
        for h in range(2):
            cols = slice(h * HALF, (h + 1) * HALF)
            xt_gw = tile("xt_gw%d" % h, [P, HALF], U32, "picked_words" if h == 0 else "w2_words")
            nc.vector.tensor_copy(xt_gw[:], xt_w[:].indirect(half_of(l1, h)))
            a_acc = psum.tile([P, HALF], F32, name="a_acc%d" % h)
            nc.tensor.matmul_mx(out=a_acc[:], lhsT=w_w[:].bitcast(E2M1), lhsT_scale=w_plane[:],
                                rhs=xt_gw[:].bitcast(E4M3), rhs_scale=xt_gs[:, cols], start=True, stop=True)
            nc.vector.tensor_copy(a_sb[:, cols], a_acc[:])
        nc.scalar.activation(pa[:].indirect(l3[:]), a_sb[:], COPY, scale=sa_t[:])

        for h in range(2):
            nc.scalar.activation(hid[h][:, 0 : 4 * HALF : 4], pa[:].indirect(half_of(l5, h)), COPY)
        for h in range(2):
            nc.scalar.activation(hid[h][:, 2 : 4 * HALF : 4], pa[:].indirect(half_of(l6, h)), COPY)
        for h in range(2):
            codes = tile("hid_codes%d" % h, [P, HALF], U32)
            scales = tile("hid_scales%d" % h, [P, HALF], U8)
            nc.vector.quantize_mx(out=codes[:].bitcast(E4M3), scales=scales[:], in_=hid[h][:])
            for t in range(2):
                rows = slice(t * P, (t + 1) * P)
                acc = psum.tile([P, HALF], F32, name="o_acc%d%d" % (h, t))
                nc.tensor.matmul_mx(out=acc[:], lhsT=wb_w[:, rows].bitcast(E5M2), lhsT_scale=wb_plane[:, rows],
                                    rhs=codes[:].bitcast(E4M3), rhs_scale=scales[:], start=True, stop=True)
                res = tile("res%d%d" % (h, t), [P, HALF], F32)
                if h == 1 and t == 1:
                    nc.scalar.activation(res[:], acc[:], COPY)
                    nc.scalar.dma_start(out[rows, h * HALF : (h + 1) * HALF], res[:])
                else:
                    nc.vector.tensor_copy(res[:], acc[:])
                    nc.sync.dma_start(out[rows, h * HALF : (h + 1) * HALF], res[:])
